import numpy as np
import ml_dtypes


def mxq(x, axis, fmt="e4m3"):
    dtype, down = {"e4m3": (ml_dtypes.float8_e4m3fn, 7), "e5m2": (ml_dtypes.float8_e5m2, 14)}[fmt]
    v = np.moveaxis(np.asarray(x, np.float32).astype(ml_dtypes.bfloat16).astype(np.float64), axis, -1)
    blocks = v.reshape(v.shape[:-1] + (-1, 32))
    amax = np.abs(blocks).max(-1, keepdims=True)
    byte = np.maximum(np.where(amax > 0, np.frexp(amax)[1] - 1 + 127, 0) - down, 1)
    scale = np.exp2(byte - 127.0)
    codes = (blocks / scale).astype(np.float32).astype(dtype).astype(np.float64)
    return np.moveaxis((codes * scale).reshape(v.shape), -1, axis)


WIDE = False


def mx_kscale(k):
    if not WIDE:
        return np.ones(k)
    levels = np.array([10, -10, 5, -5, 0])
    if k % 512:
        return np.exp2(np.random.permutation(np.resize(levels, k // 32))).repeat(32)
    a = np.empty((k // 512, 16))
    for p in range(k // 512):
        a[p, :8] = np.random.permutation(np.resize(levels, 8))
        for g in range(8):
            far = levels[np.abs(levels - a[p, g]) >= 10]
            a[p, g + 8] = far[np.random.randint(len(far))]
    return np.exp2(a.ravel()).repeat(32)


def f64(x):
    return np.asarray(x).astype(np.float64)


def striped(idx):
    return np.tile(np.asarray(idx).reshape(-1, 16).T, (8, 1)).astype(np.uint16)


def unstriped(offs):
    return offs[:16].T.reshape(-1).astype(np.int64)


D, T, J, Q, E = 512, 2048, 512, 128, 512


def setup_inputs():
    n = np.random.standard_normal
    idx = np.random.permutation(T)[:J]
    idx2 = np.random.permutation(T)[:J]
    fd = mx_kscale(D)
    fj = mx_kscale(J)
    return {
        "query": (n((D, Q)) * 0.4 / np.sqrt(D) * fd[:, None]).astype(np.float32),
        "keys": (n((D, T)) / fd[:, None]).astype(np.float32),
        "vals": (n((E, T))).astype(np.float32),
        "ka": (np.random.uniform(0.5, 1.0, (1, J))).astype(np.float32),
        "kb": (np.random.uniform(0.2, 0.7, (1, J))).astype(np.float32),
        "va": (np.random.uniform(0.5, 1.0, (1, J))).astype(np.float32),
        "vb": (np.random.uniform(0.2, 0.7, (1, J))).astype(np.float32),
        "size": (np.random.uniform(0.5, 2.0, (1, J)) * fj).astype(np.float32),
        "vsc": (np.random.uniform(0.5, 2.0, (J, 1)) / fj[:, None]).astype(np.float32),
        "offs": striped(idx),
        "offs2": striped(idx2),
    }


def reference(query, keys, vals, ka, kb, va, vb, size, vsc, offs, offs2):
    idx = unstriped(offs)
    idx2 = unstriped(offs2)
    km = f64(keys)[:, idx] * f64(ka) + f64(keys)[:, idx2] * f64(kb)
    vm = f64(vals)[:, idx] * f64(va) + f64(vals)[:, idx2] * f64(vb)
    queryq = mxq(f64(query), 0, "e4m3")
    kmq = mxq(km, 0, "e4m3")
    a = queryq.T @ kmq
    p = np.exp(a - np.max(a, axis=1, keepdims=True))
    w = p * f64(size) / np.sum(p, axis=1, keepdims=True)
    wt = w.T
    vt = vm.T
    vv = vt * f64(vsc)
    wtq = mxq(wt, 0, "e4m3")
    vvq = mxq(vv, 0, "e4m3")
    o = wtq.T @ vvq
    return o

@@ -1,0 +1,182 @@
+from contextlib import ExitStack
+
+import concourse.mybir as mybir
+from concourse.masks import make_identity
+
+D, T, J, Q, E = 512, 2048, 512, 128, 512
+FLOPS = 2 * Q * J * D + 2 * Q * J * E
+
+F32 = mybir.dt.float32
+BF16 = mybir.dt.bfloat16
+U32 = mybir.dt.uint32
+U16 = mybir.dt.uint16
+U8 = mybir.dt.uint8
+FP8X4 = mybir.dt.float8_e4m3fn_x4
+MULT = mybir.AluOpType.mult
+MAX = mybir.AluOpType.max
+EXP = mybir.ActivationFunctionType.Exp
+AXIS_X = mybir.AxisListType.X
+
+P = 128
+PACK = 4
+
+
+def tile_attend_cachemerge_kernel(tc, query, keys, vals, ka, kb, va, vb, size, vsc, offs, offs2, out):
+    nc = tc.nc
+    with ExitStack() as ctx:
+        sb = ctx.enter_context(tc.tile_pool(name="sb", bufs=1))
+        ps = ctx.enter_context(tc.psum_pool(name="ps", bufs=1))
+
+        def bank(b, shape, name):
+            return ps.tile(shape, F32, name=name, tag=f"bank{b}")
+
+        kept = sb.tile([P, J // 16], U16, name="kept")
+        evicted = sb.tile([P, J // 16], U16, name="evicted")
+        key_planes = [sb.tile([P, T], F32, name=f"key_plane{t}") for t in range(PACK)]
+        val_planes = [sb.tile([P, T], F32, name=f"val_plane{c}") for c in range(PACK)]
+        q_raw = sb.tile([P, PACK, Q], F32, name="q_raw")
+        keys_by_place = keys.rearrange("(p t) n -> t p n", t=PACK)
+
+        nc.sync.dma_start(kept[:], offs)
+        nc.sync.dma_start(key_planes[0][:], keys_by_place[0])
+        nc.sync.dma_start(evicted[:], offs2)
+        cols = {}
+        for name, vec, queue in (("ka", ka, nc.scalar), ("kb", kb, nc.scalar)):
+            cols[name] = sb.tile([P, PACK], F32, name=f"{name}_col")
+            queue.dma_start(cols[name][:], vec.rearrange("o (p t) -> p (o t)", t=PACK))
+        nc.sync.dma_start(key_planes[1][:], keys_by_place[1])
+        for name, vec in (("va", va), ("vb", vb), ("size", size)):
+            cols[name] = sb.tile([P, PACK], F32, name=f"{name}_col")
+            nc.sync.dma_start(cols[name][:], vec.rearrange("o (p t) -> p (o t)", t=PACK))
+        cols["vsc"] = sb.tile([P, PACK], F32, name="vsc_col")
+        nc.sync.dma_start(cols["vsc"][:], vsc.rearrange("(p t) o -> p (t o)", t=PACK))
+        for t in range(2, PACK):
+            nc.sync.dma_start(key_planes[t][:], keys_by_place[t])
+        nc.sync.dma_start(val_planes[0][:], vals[0:P, :])
+        nc.sync.dma_start(q_raw[:], query.rearrange("(p t) q -> p t q", t=PACK))
+        for c in range(1, PACK):
+            nc.sync.dma_start(val_planes[c][:], vals[c * P : (c + 1) * P, :])
+
+        ident = sb.tile([P, P], F32, name="ident")
+        make_identity(nc, ident[:])
+        for name in ("va", "vb"):
+            scaled = sb.tile([P, PACK], F32, name=f"{name}_scaled")
+            nc.gpsimd.tensor_tensor(scaled[:], cols[name][:], cols["vsc"][:], MULT)
+            cols[name] = scaled
+
+        def spread(name, b):
+            spread_bank = bank(b, [P, PACK, P], f"{name}_bank")
+            for t in range(PACK):
+                nc.tensor.transpose(spread_bank[:, t, :], cols[name][:, t : t + 1].to_broadcast([P, P]), ident[:])
+            return spread_bank[:].rearrange("m t n -> m n t")
+
+        rows = {}
+        for i, name in enumerate(("ka", "kb", "va", "vb")):
+            rows[name] = sb.tile([P, J], F32, name=f"{name}_row")
+            nc.scalar.copy(rows[name][:].rearrange("m (n t) -> m n t", t=PACK), spread(name, 6 + i % 2))
+
+        def gather(plane, offsets, share, name):
+            picked = sb.tile([P, J], F32, name=name)
+            nc.vector.tensor_tensor(picked[:], plane[:].indirect(offsets[:]), share[:], MULT)
+            return picked
+
+        def quantise(values, codes, scales):
+            nc.vector.quantize_mx(out=codes.bitcast(FP8X4), scales=scales, in_=values)
+
+        words_banks = [bank(4 + h, [P, 2, 2 * P], f"k_words{h}") for h in range(2)]
+        for u in range(2):
+            sum_banks = [bank(2 * u + h, [P, 2, 2, P], f"k_sum{u}{h}") for h in range(2)]
+            for e in range(2):
+                t = 2 * u + e
+                for side, (offsets, share) in enumerate(((kept, rows["ka"]), (evicted, rows["kb"]))):
+                    picked = gather(key_planes[t], offsets, share, f"k_picked{t}{side}")
+                    for b in range(PACK):
+                        nc.tensor.matmul(
+                            sum_banks[b // 2][:, b % 2, e, :],
+                            picked[:, b * P : (b + 1) * P],
+                            ident[:],
+                            start=(e == 0 and side == 0 and b % 2 == 0),
+                            stop=(e == 1 and side == 1 and b % 2 == 1),
+                            is_transpose=True,
+                        )
+            for h in range(2):
+                turned = sb.tile([P, 2, P, 2], BF16, name=f"k_turned{u}{h}")
+                nc.scalar.copy(turned[:], sum_banks[h][:].rearrange("j b e p -> j b p e"))
+                words = turned[:].rearrange("j b p e -> j (b p e)").bitcast(F32)
+                for b in range(2):
+                    nc.tensor.transpose(words_banks[h][:, u, b * P : (b + 1) * P], words[:, b * P : (b + 1) * P], ident[:])
+
+        q_grouped = sb.tile([P, Q, PACK], BF16, name="q_grouped", align_bytes=64)
+        nc.scalar.copy(q_grouped[:], q_raw[:].rearrange("p t q -> p q t"))
+        q_codes = sb.tile([P, Q], U32, name="q_codes", align_bytes=64)
+        q_scales = sb.tile([P, Q], U8, name="q_scales", align_bytes=64)
+        quantise(q_grouped[:].rearrange("p q t -> p (q t)"), q_codes[:], q_scales[:])
+
+        k_codes = sb.tile([P, J], U32, name="k_codes", align_bytes=64)
+        k_scales = sb.tile([P, J], U8, name="k_scales", align_bytes=64)
+        for h in range(2):
+            k_grouped = sb.tile([P, 2 * P * PACK], BF16, name=f"k_grouped{h}", align_bytes=64)
+            nc.scalar.copy(
+                k_grouped[:].bitcast(F32).rearrange("p (j u) -> p j u", u=2),
+                words_banks[h][:].rearrange("p u j -> p j u"),
+            )
+            half = slice(2 * P * h, 2 * P * (h + 1))
+            quantise(k_grouped[:], k_codes[:, half], k_scales[:, half])
+
+        scores = bank(6, [P, J], "scores")
+        nc.tensor.matmul_mx(
+            out=scores[:], lhsT=q_codes[:].bitcast(FP8X4), lhsT_scale=q_scales[:],
+            rhs=k_codes[:].bitcast(FP8X4), rhs_scale=k_scales[:], start=True, stop=True,
+        )
+        size_row = spread("size", 7)
+        neg_max = sb.tile([P, 1], F32, name="neg_max")
+        nc.vector.tensor_reduce(neg_max[:], scores[:], AXIS_X, MAX, negate=True)
+        probs = sb.tile([P, J], F32, name="probs")
+        row_sum = sb.tile([P, 1], F32, name="row_sum")
+        nc.scalar.activation(probs[:], scores[:], EXP, bias=neg_max[:], accum_out=row_sum[:])
+        inv_sum = sb.tile([P, 1], F32, name="inv_sum")
+        nc.vector.reciprocal(inv_sum[:], row_sum[:])
+        weights = sb.tile([P, J], BF16, name="weights")
+        nc.vector.scalar_tensor_tensor(
+            weights[:].rearrange("q (n t) -> q n t", t=PACK),
+            probs[:].rearrange("q (n t) -> q n t", t=PACK),
+            inv_sum[:], size_row, MULT, MULT,
+        )
+        w_bank = bank(4, [P, 2, Q], "w_bank")
+        w_words = weights[:].bitcast(F32)
+        for u in range(2):
+            nc.tensor.transpose(w_bank[:, u, :], w_words[:, u::2], ident[:])
+        w_grouped = sb.tile([P, Q * PACK], BF16, name="w_grouped", align_bytes=64)
+        nc.scalar.copy(w_grouped[:].bitcast(F32).rearrange("p (q u) -> p q u", u=2), w_bank[:].rearrange("p u q -> p q u"))
+        w_codes = sb.tile([P, Q], U32, name="w_codes", align_bytes=64)
+        w_scales = sb.tile([P, Q], U8, name="w_scales", align_bytes=64)
+        quantise(w_grouped[:], w_codes[:], w_scales[:])
+
+        first_out = bank(2, [P, 3 * P], "first_out")
+        last_out = bank(3, [P, P], "last_out")
+        for c in range(PACK):
+            v_bank = bank(c % 2, [P, PACK, P], f"v_sum{c}")
+            for side, (offsets, share) in enumerate(((kept, rows["va"]), (evicted, rows["vb"]))):
+                picked = gather(val_planes[c], offsets, share, f"v_picked{c}{side}")
+                for t in range(PACK):
+                    nc.tensor.matmul(
+                        v_bank[:, t, :], picked[:, t::PACK], ident[:],
+                        start=(side == 0 and t == 0), stop=(side == 1 and t == PACK - 1), is_transpose=True,
+                    )
+            v_grouped = sb.tile([P, P, PACK], BF16, name=f"v_grouped{c}", align_bytes=64)
+            nc.scalar.copy(v_grouped[:], v_bank[:].rearrange("p t e -> p e t"))
+            v_codes = sb.tile([P, P], U32, name=f"v_codes{c}", align_bytes=64)
+            v_scales = sb.tile([P, P], U8, name=f"v_scales{c}", align_bytes=64)
+            quantise(v_grouped[:].rearrange("p e t -> p (e t)"), v_codes[:], v_scales[:])
+            target = first_out[:, c * P : (c + 1) * P] if c < PACK - 1 else last_out[:]
+            nc.tensor.matmul_mx(
+                out=target, lhsT=w_codes[:].bitcast(FP8X4), lhsT_scale=w_scales[:],
+                rhs=v_codes[:].bitcast(FP8X4), rhs_scale=v_scales[:], start=True, stop=True,
+            )
+            if c == PACK - 2:
+                first_sb = sb.tile([P, 3 * P], F32, name="first_sb")
+                nc.scalar.copy(first_sb[:], first_out[:])
+                nc.sync.dma_start(out[:, 0 : 3 * P], first_sb[:])
+        last_sb = sb.tile([P, P], F32, name="last_sb")
+        nc.vector.tensor_copy(last_sb[:], last_out[:])
+        nc.sync.dma_start(out[:, 3 * P :], last_sb[:])

@@ -13,6 +13,7 @@ U16 = mybir.dt.uint16
 U8 = mybir.dt.uint8
 FP8X4 = mybir.dt.float8_e4m3fn_x4
 MULT = mybir.AluOpType.mult
+ADD = mybir.AluOpType.add
 MAX = mybir.AluOpType.max
 EXP = mybir.ActivationFunctionType.Exp
 AXIS_X = mybir.AxisListType.X
@@ -52,9 +53,8 @@ def tile_attend_cachemerge_kernel(tc, query, keys, vals, ka, kb, va, vb, size, v
         nc.sync.dma_start(cols["vsc"][:], vsc.rearrange("(p t) o -> p (t o)", t=PACK))
         for t in range(2, PACK):
             nc.sync.dma_start(key_planes[t][:], keys_by_place[t])
-        nc.sync.dma_start(val_planes[0][:], vals[0:P, :])
         nc.sync.dma_start(q_raw[:], query.rearrange("(p t) q -> p t q", t=PACK))
-        for c in range(1, PACK):
+        for c in range(PACK):
             nc.sync.dma_start(val_planes[c][:], vals[c * P : (c + 1) * P, :])
 
         ident = sb.tile([P, P], F32, name="ident")
@@ -155,19 +155,24 @@ def tile_attend_cachemerge_kernel(tc, query, keys, vals, ka, kb, va, vb, size, v
         first_out = bank(2, [P, 3 * P], "first_out")
         last_out = bank(3, [P, P], "last_out")
         for c in range(PACK):
-            v_bank = bank(c % 2, [P, PACK, P], f"v_sum{c}")
-            for side, (offsets, share) in enumerate(((kept, rows["va"]), (evicted, rows["vb"]))):
-                picked = gather(val_planes[c], offsets, share, f"v_picked{c}{side}")
-                for t in range(PACK):
-                    nc.tensor.matmul(
-                        v_bank[:, t, :], picked[:, t::PACK], ident[:],
-                        start=(side == 0 and t == 0), stop=(side == 1 and t == PACK - 1), is_transpose=True,
-                    )
-            v_grouped = sb.tile([P, P, PACK], BF16, name=f"v_grouped{c}", align_bytes=64)
-            nc.scalar.copy(v_grouped[:], v_bank[:].rearrange("p t e -> p e t"))
+            kept_part = gather(val_planes[c], kept, rows["va"], f"v_kept{c}")
+            evicted_part = gather(val_planes[c], evicted, rows["vb"], f"v_evicted{c}")
+            merged = sb.tile([P, 2, P, 2], BF16, name=f"v_merged{c}")
+            nc.vector.tensor_tensor(
+                merged[:],
+                kept_part[:].rearrange("e (s u i) -> e u s i", u=2, i=2),
+                evicted_part[:].rearrange("e (s u i) -> e u s i", u=2, i=2),
+                ADD,
+            )
+            v_words = merged[:].rearrange("e u s i -> e (u s i)").bitcast(F32)
+            v_bank = bank(c % 2, [P, 2, P], f"v_words{c}")
+            for u in range(2):
+                nc.tensor.transpose(v_bank[:, u, :], v_words[:, u * P : (u + 1) * P], ident[:])
+            v_grouped = sb.tile([P, P * PACK], BF16, name=f"v_grouped{c}", align_bytes=64)
+            nc.scalar.copy(v_grouped[:].bitcast(F32).rearrange("p (e u) -> p e u", u=2), v_bank[:].rearrange("p u e -> p e u"))
             v_codes = sb.tile([P, P], U32, name=f"v_codes{c}", align_bytes=64)
             v_scales = sb.tile([P, P], U8, name=f"v_scales{c}", align_bytes=64)
-            quantise(v_grouped[:].rearrange("p e t -> p (e t)"), v_codes[:], v_scales[:])
+            quantise(v_grouped[:], v_codes[:], v_scales[:])
             target = first_out[:, c * P : (c + 1) * P] if c < PACK - 1 else last_out[:]
             nc.tensor.matmul_mx(
                 out=target, lhsT=w_codes[:].bitcast(FP8X4), lhsT_scale=w_scales[:],

@@ -15,6 +15,7 @@ FP8X4 = mybir.dt.float8_e4m3fn_x4
 MULT = mybir.AluOpType.mult
 ADD = mybir.AluOpType.add
 MAX = mybir.AluOpType.max
+COPY = mybir.ActivationFunctionType.Copy
 EXP = mybir.ActivationFunctionType.Exp
 AXIS_X = mybir.AxisListType.X
 
@@ -42,15 +43,17 @@ def tile_attend_cachemerge_kernel(tc, query, keys, vals, ka, kb, va, vb, size, v
         nc.sync.dma_start(key_planes[0][:], keys_by_place[0])
         nc.sync.dma_start(evicted[:], offs2)
         cols = {}
-        for name, vec, queue in (("ka", ka, nc.scalar), ("kb", kb, nc.scalar)):
+        vsc_row = vsc.rearrange("j o -> o j")
+
+        def load_column(queue, name, vec):
             cols[name] = sb.tile([P, PACK], F32, name=f"{name}_col")
             queue.dma_start(cols[name][:], vec.rearrange("o (p t) -> p (o t)", t=PACK))
+
+        load_column(nc.scalar, "ka", ka)
+        load_column(nc.scalar, "kb", kb)
         nc.sync.dma_start(key_planes[1][:], keys_by_place[1])
-        for name, vec in (("va", va), ("vb", vb), ("size", size)):
-            cols[name] = sb.tile([P, PACK], F32, name=f"{name}_col")
-            nc.sync.dma_start(cols[name][:], vec.rearrange("o (p t) -> p (o t)", t=PACK))
-        cols["vsc"] = sb.tile([P, PACK], F32, name="vsc_col")
-        nc.sync.dma_start(cols["vsc"][:], vsc.rearrange("(p t) o -> p (t o)", t=PACK))
+        for name, vec in (("va", va), ("vb", vb), ("vsc", vsc_row), ("size", size)):
+            load_column(nc.sync, name, vec)
         for t in range(2, PACK):
             nc.sync.dma_start(key_planes[t][:], keys_by_place[t])
         nc.sync.dma_start(q_raw[:], query.rearrange("(p t) q -> p t q", t=PACK))
@@ -59,11 +62,6 @@ def tile_attend_cachemerge_kernel(tc, query, keys, vals, ka, kb, va, vb, size, v
 
         ident = sb.tile([P, P], F32, name="ident")
         make_identity(nc, ident[:])
-        for name in ("va", "vb"):
-            scaled = sb.tile([P, PACK], F32, name=f"{name}_scaled")
-            nc.gpsimd.tensor_tensor(scaled[:], cols[name][:], cols["vsc"][:], MULT)
-            cols[name] = scaled
-
         def spread(name, b):
             spread_bank = bank(b, [P, PACK, P], f"{name}_bank")
             for t in range(PACK):
@@ -71,9 +69,21 @@ def tile_attend_cachemerge_kernel(tc, query, keys, vals, ka, kb, va, vb, size, v
             return spread_bank[:].rearrange("m t n -> m n t")
 
         rows = {}
-        for i, name in enumerate(("ka", "kb", "va", "vb")):
+
+        def share_row(name, b):
             rows[name] = sb.tile([P, J], F32, name=f"{name}_row")
-            nc.scalar.copy(rows[name][:].rearrange("m (n t) -> m n t", t=PACK), spread(name, 6 + i % 2))
+            nc.scalar.copy(rows[name][:].rearrange("m (n t) -> m n t", t=PACK), spread(name, b))
+
+        share_row("ka", 6)
+        share_row("kb", 7)
+        for name in ("va", "vb"):
+            scaled = sb.tile([P, PACK], F32, name=f"{name}_scaled")
+            for t in range(PACK):
+                nc.scalar.activation(scaled[:, t : t + 1], cols[name][:, t : t + 1], COPY, scale=cols["vsc"][:, t : t + 1])
+            cols[name] = scaled
+
+        share_row("va", 6)
+        share_row("vb", 7)
 
         def gather(plane, offsets, share, name):
             picked = sb.tile([P, J], F32, name=name)

@@ -68,22 +68,26 @@ def tile_attend_cachemerge_kernel(tc, query, keys, vals, ka, kb, va, vb, size, v
                 nc.tensor.transpose(spread_bank[:, t, :], cols[name][:, t : t + 1].to_broadcast([P, P]), ident[:])
             return spread_bank[:].rearrange("m t n -> m n t")
 
-        rows = {}
+        def share_rows(name, b, tags):
+            spread_view = spread(name, b)
+            copies = []
+            for tag in tags:
+                row = sb.tile([P, J], F32, name=tag, tag=tag, align_bytes=64)
+                nc.scalar.copy(row[:].rearrange("m (n t) -> m n t", t=PACK), spread_view)
+                copies.append(row)
+            return copies
 
-        def share_row(name, b):
-            rows[name] = sb.tile([P, J], F32, name=f"{name}_row")
-            nc.scalar.copy(rows[name][:].rearrange("m (n t) -> m n t", t=PACK), spread(name, b))
-
-        share_row("ka", 6)
-        share_row("kb", 7)
+        (ka_row,) = share_rows("ka", 6, ["ka_row"])
+        (kb_row,) = share_rows("kb", 7, ["kb_row"])
         for name in ("va", "vb"):
             scaled = sb.tile([P, PACK], F32, name=f"{name}_scaled")
             for t in range(PACK):
                 nc.scalar.activation(scaled[:, t : t + 1], cols[name][:, t : t + 1], COPY, scale=cols["vsc"][:, t : t + 1])
             cols[name] = scaled
-
-        share_row("va", 6)
-        share_row("vb", 7)
+        va_tags = ["va_early", "va_late"]
+        va_copies = share_rows("va", 6, va_tags)
+        va_rows = [va_copies[i] for i in (0, 0, 1, 1)]
+        (vb_row,) = share_rows("vb", 7, ["vb_row"])
 
         def gather(plane, offsets, share, name):
             picked = sb.tile([P, J], F32, name=name)
@@ -98,7 +102,7 @@ def tile_attend_cachemerge_kernel(tc, query, keys, vals, ka, kb, va, vb, size, v
             sum_banks = [bank(2 * u + h, [P, 2, 2, P], f"k_sum{u}{h}") for h in range(2)]
             for e in range(2):
                 t = 2 * u + e
-                for side, (offsets, share) in enumerate(((kept, rows["ka"]), (evicted, rows["kb"]))):
+                for side, (offsets, share) in enumerate(((kept, ka_row), (evicted, kb_row))):
                     picked = gather(key_planes[t], offsets, share, f"k_picked{t}{side}")
                     for b in range(PACK):
                         nc.tensor.matmul(
@@ -122,30 +126,67 @@ def tile_attend_cachemerge_kernel(tc, query, keys, vals, ka, kb, va, vb, size, v
         q_scales = sb.tile([P, Q], U8, name="q_scales", align_bytes=64)
         quantise(q_grouped[:].rearrange("p q t -> p (q t)"), q_codes[:], q_scales[:])
 
-        k_codes = sb.tile([P, J], U32, name="k_codes", align_bytes=64)
-        k_scales = sb.tile([P, J], U8, name="k_scales", align_bytes=64)
+        k_grouped = sb.tile([P, J * PACK], BF16, name="k_grouped", align_bytes=64)
+        k_words = k_grouped[:].bitcast(F32).rearrange("p (j u) -> p j u", u=2)
         for h in range(2):
-            k_grouped = sb.tile([P, 2 * P * PACK], BF16, name=f"k_grouped{h}", align_bytes=64)
-            nc.scalar.copy(
-                k_grouped[:].bitcast(F32).rearrange("p (j u) -> p j u", u=2),
-                words_banks[h][:].rearrange("p u j -> p j u"),
-            )
-            half = slice(2 * P * h, 2 * P * (h + 1))
-            quantise(k_grouped[:], k_codes[:, half], k_scales[:, half])
+            nc.scalar.copy(k_words[:, 2 * P * h : 2 * P * (h + 1), :], words_banks[h][:].rearrange("p u j -> p j u"))
+        size_row = spread("size", 7)
 
+        v_banks = {}
+        v_grouped = {}
+        v_quantised = {}
+
+        def turn_values(c, side):
+            offsets, share = ((kept, va_rows[c]), (evicted, vb_row))[side]
+            picked = gather(val_planes[c], offsets, share, f"v_picked{c}{side}")
+            dealt = sb.tile([P, PACK, P], F32, name=f"v_dealt{c}{side}")
+            nc.scalar.copy(dealt[:].rearrange("e t s -> e s t"), picked[:].rearrange("e (s t) -> e s t", t=PACK))
+            if side == 0:
+                v_banks[c] = bank(c % 2, [P, PACK, P], f"v_sum{c}")
+            for t in range(PACK):
+                nc.tensor.matmul(
+                    v_banks[c][:, t, :], dealt[:, t, :], ident[:],
+                    start=(side == 0 and t == 0), stop=(side == 1 and t == PACK - 1), is_transpose=True,
+                )
+            if side == 1:
+                v_grouped[c] = sb.tile([P, P * PACK], BF16, name=f"v_grouped{c}", align_bytes=64)
+                nc.scalar.copy(v_grouped[c][:].rearrange("p (e t) -> p e t", t=PACK), v_banks[c][:].rearrange("p t e -> p e t"))
+
+        def quantise_values(c):
+            v_codes = sb.tile([P, P], U32, name=f"v_codes{c}", align_bytes=64)
+            v_scales = sb.tile([P, P], U8, name=f"v_scales{c}", align_bytes=64)
+            quantise(v_grouped[c][:], v_codes[:], v_scales[:])
+            v_quantised[c] = (v_codes, v_scales)
+
+        def weigh_values(c, target):
+            v_codes, v_scales = v_quantised[c]
+            nc.tensor.matmul_mx(
+                out=target, lhsT=w_codes[:].bitcast(FP8X4), lhsT_scale=w_scales[:],
+                rhs=v_codes[:].bitcast(FP8X4), rhs_scale=v_scales[:], start=True, stop=True,
+            )
+
+        turn_values(0, 0)
+        turn_values(0, 1)
+        turn_values(1, 0)
+        k_codes = sb.tile([P, J], U32, name="k_codes", tag=va_tags[0], align_bytes=64)
+        k_scales = sb.tile([P, J], U8, name="k_scales", align_bytes=64)
+        quantise(k_grouped[:], k_codes[:], k_scales[:])
         scores = bank(6, [P, J], "scores")
         nc.tensor.matmul_mx(
             out=scores[:], lhsT=q_codes[:].bitcast(FP8X4), lhsT_scale=q_scales[:],
             rhs=k_codes[:].bitcast(FP8X4), rhs_scale=k_scales[:], start=True, stop=True,
         )
-        size_row = spread("size", 7)
-        neg_max = sb.tile([P, 1], F32, name="neg_max")
+        turn_values(1, 1)
+        neg_max = sb.tile([P, 1], F32, name="neg_max", align_bytes=64)
         nc.vector.tensor_reduce(neg_max[:], scores[:], AXIS_X, MAX, negate=True)
         probs = sb.tile([P, J], F32, name="probs")
         row_sum = sb.tile([P, 1], F32, name="row_sum")
         nc.scalar.activation(probs[:], scores[:], EXP, bias=neg_max[:], accum_out=row_sum[:])
+        turn_values(2, 0)
+        turn_values(2, 1)
         inv_sum = sb.tile([P, 1], F32, name="inv_sum")
         nc.vector.reciprocal(inv_sum[:], row_sum[:])
+        quantise_values(0)
         weights = sb.tile([P, J], BF16, name="weights")
         nc.vector.scalar_tensor_tensor(
             weights[:].rearrange("q (n t) -> q n t", t=PACK),
@@ -158,40 +199,43 @@ def tile_attend_cachemerge_kernel(tc, query, keys, vals, ka, kb, va, vb, size, v
             nc.tensor.transpose(w_bank[:, u, :], w_words[:, u::2], ident[:])
         w_grouped = sb.tile([P, Q * PACK], BF16, name="w_grouped", align_bytes=64)
         nc.scalar.copy(w_grouped[:].bitcast(F32).rearrange("p (q u) -> p q u", u=2), w_bank[:].rearrange("p u q -> p q u"))
+
+        last = PACK - 1
+        kept_part = gather(val_planes[last], kept, va_rows[last], "v_kept")
+        quantise_values(1)
+        evicted_part = gather(val_planes[last], evicted, vb_row, "v_evicted")
         w_codes = sb.tile([P, Q], U32, name="w_codes", align_bytes=64)
         w_scales = sb.tile([P, Q], U8, name="w_scales", align_bytes=64)
         quantise(w_grouped[:], w_codes[:], w_scales[:])
-
-        first_out = bank(2, [P, 3 * P], "first_out")
-        last_out = bank(3, [P, P], "last_out")
-        for c in range(PACK):
-            kept_part = gather(val_planes[c], kept, rows["va"], f"v_kept{c}")
-            evicted_part = gather(val_planes[c], evicted, rows["vb"], f"v_evicted{c}")
-            merged = sb.tile([P, 2, P, 2], BF16, name=f"v_merged{c}")
+        first_out = bank(2, [P, 2 * P], "first_out")
+        for c in range(2):
+            weigh_values(c, first_out[:, c * P : (c + 1) * P])
+        first_sb = sb.tile([P, 2 * P], F32, name="first_sb")
+        nc.scalar.copy(first_sb[:], first_out[:])
+        nc.sync.dma_start(out[:, 0 : 2 * P], first_sb[:])
+        merged = sb.tile([P, 2, P, 2], BF16, name="v_merged")
+        for u in range(2):
             nc.vector.tensor_tensor(
-                merged[:],
-                kept_part[:].rearrange("e (s u i) -> e u s i", u=2, i=2),
-                evicted_part[:].rearrange("e (s u i) -> e u s i", u=2, i=2),
+                merged[:, u],
+                kept_part[:].rearrange("e (s u i) -> e u s i", u=2, i=2)[:, u],
+                evicted_part[:].rearrange("e (s u i) -> e u s i", u=2, i=2)[:, u],
                 ADD,
             )
-            v_words = merged[:].rearrange("e u s i -> e (u s i)").bitcast(F32)
-            v_bank = bank(c % 2, [P, 2, P], f"v_words{c}")
-            for u in range(2):
-                nc.tensor.transpose(v_bank[:, u, :], v_words[:, u * P : (u + 1) * P], ident[:])
-            v_grouped = sb.tile([P, P * PACK], BF16, name=f"v_grouped{c}", align_bytes=64)
-            nc.scalar.copy(v_grouped[:].bitcast(F32).rearrange("p (e u) -> p e u", u=2), v_bank[:].rearrange("p u e -> p e u"))
-            v_codes = sb.tile([P, P], U32, name=f"v_codes{c}", align_bytes=64)
-            v_scales = sb.tile([P, P], U8, name=f"v_scales{c}", align_bytes=64)
-            quantise(v_grouped[:], v_codes[:], v_scales[:])
-            target = first_out[:, c * P : (c + 1) * P] if c < PACK - 1 else last_out[:]
-            nc.tensor.matmul_mx(
-                out=target, lhsT=w_codes[:].bitcast(FP8X4), lhsT_scale=w_scales[:],
-                rhs=v_codes[:].bitcast(FP8X4), rhs_scale=v_scales[:], start=True, stop=True,
-            )
-            if c == PACK - 2:
-                first_sb = sb.tile([P, 3 * P], F32, name="first_sb")
-                nc.scalar.copy(first_sb[:], first_out[:])
-                nc.sync.dma_start(out[:, 0 : 3 * P], first_sb[:])
+        v_words = merged[:].rearrange("e u s i -> e (u s i)").bitcast(F32)
+        v_bank = bank(5, [P, 2, P], "v_words")
+        for u in range(2):
+            nc.tensor.transpose(v_bank[:, u, :], v_words[:, u * P : (u + 1) * P], ident[:])
+        v_grouped[last] = sb.tile([P, P * PACK], BF16, name="v_grouped_last", align_bytes=64)
+        nc.scalar.copy(v_grouped[last][:].bitcast(F32).rearrange("p (e u) -> p e u", u=2), v_bank[:].rearrange("p u e -> p e u"))
+        quantise_values(2)
+        third_out = bank(4, [P, P], "third_out")
+        weigh_values(2, third_out[:])
+        third_sb = sb.tile([P, P], F32, name="third_sb")
+        nc.scalar.copy(third_sb[:], third_out[:])
+        nc.sync.dma_start(out[:, 2 * P : 3 * P], third_sb[:])
+        quantise_values(last)
+        last_out = bank(3, [P, P], "last_out")
+        weigh_values(last, last_out[:])
         last_sb = sb.tile([P, P], F32, name="last_sb")
         nc.vector.tensor_copy(last_sb[:], last_out[:])
-        nc.sync.dma_start(out[:, 3 * P :], last_sb[:])
+        nc.sync.dma_start(out[:, last * P :], last_sb[:])

from contextlib import ExitStack

import concourse.mybir as mybir
from concourse.masks import make_identity

D, T, J, Q, E = 512, 2048, 512, 128, 512
FLOPS = 2 * Q * J * D + 2 * Q * J * E

F32 = mybir.dt.float32
BF16 = mybir.dt.bfloat16
U32 = mybir.dt.uint32
U16 = mybir.dt.uint16
U8 = mybir.dt.uint8
FP8X4 = mybir.dt.float8_e4m3fn_x4
MULT = mybir.AluOpType.mult
ADD = mybir.AluOpType.add
MAX = mybir.AluOpType.max
COPY = mybir.ActivationFunctionType.Copy
EXP = mybir.ActivationFunctionType.Exp
AXIS_X = mybir.AxisListType.X

P = 128
PACK = 4


def tile_attend_cachemerge_kernel(tc, query, keys, vals, ka, kb, va, vb, size, vsc, offs, offs2, out):
    nc = tc.nc
    with ExitStack() as ctx:
        sb = ctx.enter_context(tc.tile_pool(name="sb", bufs=1))
        ps = ctx.enter_context(tc.psum_pool(name="ps", bufs=1))

        def bank(b, shape, name):
            return ps.tile(shape, F32, name=name, tag=f"bank{b}")

        kept = sb.tile([P, J // 16], U16, name="kept")
        evicted = sb.tile([P, J // 16], U16, name="evicted")
        key_planes = [sb.tile([P, T], F32, name=f"key_plane{t}") for t in range(PACK)]
        val_planes = [sb.tile([P, T], F32, name=f"val_plane{c}") for c in range(PACK)]
        q_raw = sb.tile([P, PACK, Q], F32, name="q_raw")
        keys_by_place = keys.rearrange("(p t) n -> t p n", t=PACK)

        nc.sync.dma_start(kept[:], offs)
        nc.sync.dma_start(key_planes[0][:], keys_by_place[0])
        nc.sync.dma_start(evicted[:], offs2)
        cols = {}
        vsc_row = vsc.rearrange("j o -> o j")

        def load_column(queue, name, vec):
            cols[name] = sb.tile([P, PACK], F32, name=f"{name}_col")
            queue.dma_start(cols[name][:], vec.rearrange("o (p t) -> p (o t)", t=PACK))

        load_column(nc.scalar, "ka", ka)
        load_column(nc.scalar, "kb", kb)
        nc.sync.dma_start(key_planes[1][:], keys_by_place[1])
        for name, vec in (("va", va), ("vb", vb), ("vsc", vsc_row), ("size", size)):
            load_column(nc.sync, name, vec)
        for t in range(2, PACK):
            nc.sync.dma_start(key_planes[t][:], keys_by_place[t])
        nc.sync.dma_start(q_raw[:], query.rearrange("(p t) q -> p t q", t=PACK))
        for c in range(PACK):
            nc.sync.dma_start(val_planes[c][:], vals[c * P : (c + 1) * P, :])

        ident = sb.tile([P, P], F32, name="ident")
        make_identity(nc, ident[:])
        def spread(name, b):
            spread_bank = bank(b, [P, PACK, P], f"{name}_bank")
            for t in range(PACK):
                nc.tensor.transpose(spread_bank[:, t, :], cols[name][:, t : t + 1].to_broadcast([P, P]), ident[:])
            return spread_bank[:].rearrange("m t n -> m n t")

        def share_rows(name, b, tags):
            spread_view = spread(name, b)
            copies = []
            for tag in tags:
                row = sb.tile([P, J], F32, name=tag, tag=tag, align_bytes=64)
                nc.scalar.copy(row[:].rearrange("m (n t) -> m n t", t=PACK), spread_view)
                copies.append(row)
            return copies

        (ka_row,) = share_rows("ka", 6, ["ka_row"])
        (kb_row,) = share_rows("kb", 7, ["kb_row"])
        for name in ("va", "vb"):
            scaled = sb.tile([P, PACK], F32, name=f"{name}_scaled")
            for t in range(PACK):
                nc.scalar.activation(scaled[:, t : t + 1], cols[name][:, t : t + 1], COPY, scale=cols["vsc"][:, t : t + 1])
            cols[name] = scaled
        va_tags = ["va_early", "va_late"]
        va_copies = share_rows("va", 6, va_tags)
        va_rows = [va_copies[i] for i in (0, 0, 1, 1)]
        (vb_row,) = share_rows("vb", 7, ["vb_row"])

        def gather(plane, offsets, share, name):
            picked = sb.tile([P, J], F32, name=name)
            nc.vector.tensor_tensor(picked[:], plane[:].indirect(offsets[:]), share[:], MULT)
            return picked

        def quantise(values, codes, scales):
            nc.vector.quantize_mx(out=codes.bitcast(FP8X4), scales=scales, in_=values)

        words_banks = [bank(4 + h, [P, 2, 2 * P], f"k_words{h}") for h in range(2)]
        for u in range(2):
            sum_banks = [bank(2 * u + h, [P, 2, 2, P], f"k_sum{u}{h}") for h in range(2)]
            for e in range(2):
                t = 2 * u + e
                for side, (offsets, share) in enumerate(((kept, ka_row), (evicted, kb_row))):
                    picked = gather(key_planes[t], offsets, share, f"k_picked{t}{side}")
                    for b in range(PACK):
                        nc.tensor.matmul(
                            sum_banks[b // 2][:, b % 2, e, :],
                            picked[:, b * P : (b + 1) * P],
                            ident[:],
                            start=(e == 0 and side == 0 and b % 2 == 0),
                            stop=(e == 1 and side == 1 and b % 2 == 1),
                            is_transpose=True,
                        )
            for h in range(2):
                turned = sb.tile([P, 2, P, 2], BF16, name=f"k_turned{u}{h}")
                nc.scalar.copy(turned[:], sum_banks[h][:].rearrange("j b e p -> j b p e"))
                words = turned[:].rearrange("j b p e -> j (b p e)").bitcast(F32)
                for b in range(2):
                    nc.tensor.transpose(words_banks[h][:, u, b * P : (b + 1) * P], words[:, b * P : (b + 1) * P], ident[:])

        q_grouped = sb.tile([P, Q, PACK], BF16, name="q_grouped", align_bytes=64)
        nc.scalar.copy(q_grouped[:], q_raw[:].rearrange("p t q -> p q t"))
        q_codes = sb.tile([P, Q], U32, name="q_codes", align_bytes=64)
        q_scales = sb.tile([P, Q], U8, name="q_scales", align_bytes=64)
        quantise(q_grouped[:].rearrange("p q t -> p (q t)"), q_codes[:], q_scales[:])

        k_grouped = sb.tile([P, J * PACK], BF16, name="k_grouped", align_bytes=64)
        k_words = k_grouped[:].bitcast(F32).rearrange("p (j u) -> p j u", u=2)
        for h in range(2):
            nc.scalar.copy(k_words[:, 2 * P * h : 2 * P * (h + 1), :], words_banks[h][:].rearrange("p u j -> p j u"))
        size_row = spread("size", 7)

        v_banks = {}
        v_grouped = {}
        v_quantised = {}

        def turn_values(c, side):
            offsets, share = ((kept, va_rows[c]), (evicted, vb_row))[side]
            picked = gather(val_planes[c], offsets, share, f"v_picked{c}{side}")
            dealt = sb.tile([P, PACK, P], F32, name=f"v_dealt{c}{side}")
            nc.scalar.copy(dealt[:].rearrange("e t s -> e s t"), picked[:].rearrange("e (s t) -> e s t", t=PACK))
            if side == 0:
                v_banks[c] = bank(c % 2, [P, PACK, P], f"v_sum{c}")
            for t in range(PACK):
                nc.tensor.matmul(
                    v_banks[c][:, t, :], dealt[:, t, :], ident[:],
                    start=(side == 0 and t == 0), stop=(side == 1 and t == PACK - 1), is_transpose=True,
                )
            if side == 1:
                v_grouped[c] = sb.tile([P, P * PACK], BF16, name=f"v_grouped{c}", align_bytes=64)
                nc.scalar.copy(v_grouped[c][:].rearrange("p (e t) -> p e t", t=PACK), v_banks[c][:].rearrange("p t e -> p e t"))

        def quantise_values(c):
            v_codes = sb.tile([P, P], U32, name=f"v_codes{c}", align_bytes=64)
            v_scales = sb.tile([P, P], U8, name=f"v_scales{c}", align_bytes=64)
            quantise(v_grouped[c][:], v_codes[:], v_scales[:])
            v_quantised[c] = (v_codes, v_scales)

        def weigh_values(c, target):
            v_codes, v_scales = v_quantised[c]
            nc.tensor.matmul_mx(
                out=target, lhsT=w_codes[:].bitcast(FP8X4), lhsT_scale=w_scales[:],
                rhs=v_codes[:].bitcast(FP8X4), rhs_scale=v_scales[:], start=True, stop=True,
            )

        turn_values(0, 0)
        turn_values(0, 1)
        turn_values(1, 0)
        k_codes = sb.tile([P, J], U32, name="k_codes", tag=va_tags[0], align_bytes=64)
        k_scales = sb.tile([P, J], U8, name="k_scales", align_bytes=64)
        quantise(k_grouped[:], k_codes[:], k_scales[:])
        scores = bank(6, [P, J], "scores")
        nc.tensor.matmul_mx(
            out=scores[:], lhsT=q_codes[:].bitcast(FP8X4), lhsT_scale=q_scales[:],
            rhs=k_codes[:].bitcast(FP8X4), rhs_scale=k_scales[:], start=True, stop=True,
        )
        turn_values(1, 1)
        neg_max = sb.tile([P, 1], F32, name="neg_max", align_bytes=64)
        nc.vector.tensor_reduce(neg_max[:], scores[:], AXIS_X, MAX, negate=True)
        probs = sb.tile([P, J], F32, name="probs")
        row_sum = sb.tile([P, 1], F32, name="row_sum")
        nc.scalar.activation(probs[:], scores[:], EXP, bias=neg_max[:], accum_out=row_sum[:])
        turn_values(2, 0)
        turn_values(2, 1)
        inv_sum = sb.tile([P, 1], F32, name="inv_sum")
        nc.vector.reciprocal(inv_sum[:], row_sum[:])
        quantise_values(0)
        weights = sb.tile([P, J], BF16, name="weights")
        nc.vector.scalar_tensor_tensor(
            weights[:].rearrange("q (n t) -> q n t", t=PACK),
            probs[:].rearrange("q (n t) -> q n t", t=PACK),
            inv_sum[:], size_row, MULT, MULT,
        )
        w_bank = bank(4, [P, 2, Q], "w_bank")
        w_words = weights[:].bitcast(F32)
        for u in range(2):
            nc.tensor.transpose(w_bank[:, u, :], w_words[:, u::2], ident[:])
        w_grouped = sb.tile([P, Q * PACK], BF16, name="w_grouped", align_bytes=64)
        nc.scalar.copy(w_grouped[:].bitcast(F32).rearrange("p (q u) -> p q u", u=2), w_bank[:].rearrange("p u q -> p q u"))

        last = PACK - 1
        kept_part = gather(val_planes[last], kept, va_rows[last], "v_kept")
        quantise_values(1)
        evicted_part = gather(val_planes[last], evicted, vb_row, "v_evicted")
        w_codes = sb.tile([P, Q], U32, name="w_codes", align_bytes=64)
        w_scales = sb.tile([P, Q], U8, name="w_scales", align_bytes=64)
        quantise(w_grouped[:], w_codes[:], w_scales[:])
        first_out = bank(2, [P, 2 * P], "first_out")
        for c in range(2):
            weigh_values(c, first_out[:, c * P : (c + 1) * P])
        first_sb = sb.tile([P, 2 * P], F32, name="first_sb")
        nc.scalar.copy(first_sb[:], first_out[:])
        nc.sync.dma_start(out[:, 0 : 2 * P], first_sb[:])
        merged = sb.tile([P, 2, P, 2], BF16, name="v_merged")
        for u in range(2):
            nc.vector.tensor_tensor(
                merged[:, u],
                kept_part[:].rearrange("e (s u i) -> e u s i", u=2, i=2)[:, u],
                evicted_part[:].rearrange("e (s u i) -> e u s i", u=2, i=2)[:, u],
                ADD,
            )
        v_words = merged[:].rearrange("e u s i -> e (u s i)").bitcast(F32)
        v_bank = bank(5, [P, 2, P], "v_words")
        for u in range(2):
            nc.tensor.transpose(v_bank[:, u, :], v_words[:, u * P : (u + 1) * P], ident[:])
        v_grouped[last] = sb.tile([P, P * PACK], BF16, name="v_grouped_last", align_bytes=64)
        nc.scalar.copy(v_grouped[last][:].bitcast(F32).rearrange("p (e u) -> p e u", u=2), v_bank[:].rearrange("p u e -> p e u"))
        quantise_values(2)
        third_out = bank(4, [P, P], "third_out")
        weigh_values(2, third_out[:])
        third_sb = sb.tile([P, P], F32, name="third_sb")
        nc.scalar.copy(third_sb[:], third_out[:])
        nc.sync.dma_start(out[:, 2 * P : 3 * P], third_sb[:])
        quantise_values(last)
        last_out = bank(3, [P, P], "last_out")
        weigh_values(last, last_out[:])
        last_sb = sb.tile([P, P], F32, name="last_sb")
        nc.vector.tensor_copy(last_sb[:], last_out[:])
        nc.sync.dma_start(out[:, last * P :], last_sb[:])
